import numpy as np
import ml_dtypes


def mxq(x, axis, fmt="e4m3"):
    dtype, down = {"e4m3": (ml_dtypes.float8_e4m3fn, 7), "e5m2": (ml_dtypes.float8_e5m2, 14)}[fmt]
    v = np.moveaxis(np.asarray(x, np.float32).astype(ml_dtypes.bfloat16).astype(np.float64), axis, -1)
    blocks = v.reshape(v.shape[:-1] + (-1, 32))
    amax = np.abs(blocks).max(-1, keepdims=True)
    byte = np.maximum(np.where(amax > 0, np.frexp(amax)[1] - 1 + 127, 0) - down, 1)
    scale = np.exp2(byte - 127.0)
    codes = (blocks / scale).astype(np.float32).astype(dtype).astype(np.float64)
    return np.moveaxis((codes * scale).reshape(v.shape), -1, axis)


WIDE = False


def mx_kscale(k):
    if not WIDE:
        return np.ones(k)
    levels = np.array([10, -10, 5, -5, 0])
    if k % 512:
        return np.exp2(np.random.permutation(np.resize(levels, k // 32))).repeat(32)
    a = np.empty((k // 512, 16))
    for p in range(k // 512):
        a[p, :8] = np.random.permutation(np.resize(levels, 8))
        for g in range(8):
            far = levels[np.abs(levels - a[p, g]) >= 10]
            a[p, g + 8] = far[np.random.randint(len(far))]
    return np.exp2(a.ravel()).repeat(32)


def f64(x):
    return np.asarray(x).astype(np.float64)


def striped(idx):
    return np.tile(idx.reshape(-1, 16).T, (8, 1)).astype(np.uint16)


def unstriped(offs):
    return offs[:16].T.reshape(-1).astype(np.int64)


E2M1 = np.array([0.0, 0.5, 1.0, 1.5, 2.0, 3.0, 4.0, 6.0, -0.0, -0.5, -1.0, -1.5, -2.0, -3.0, -4.0, -6.0])


def pack_weight(w, fmt):
    k, n = w.shape
    w = f64(np.asarray(w, np.float32).astype(ml_dtypes.bfloat16)).reshape(k // 32, 32, n)
    amax = np.abs(w).max(1)
    if fmt == "e4m3":
        byte = np.frexp(amax)[1] - 1 + 127 - 7
    else:
        mant, ex = np.frexp(amax / 6.0)
        byte = np.where(mant > 0.5, ex, ex - 1) + 127
    byte = np.clip(np.where(amax > 0, byte, 1), 1, 254)
    scaled = (w * np.exp2(127.0 - byte)[:, None, :]).reshape(k, n).astype(np.float32)
    by_word = np.ascontiguousarray(scaled.reshape(k // 512, 128, 4, n).transpose(0, 1, 3, 2))
    if fmt == "e4m3":
        words = by_word.astype(ml_dtypes.float8_e4m3fn).view(np.uint8)
    else:
        c = by_word.astype(ml_dtypes.float4_e2m1fn).view(np.uint8) & 0xF
        words = (c[..., 0::2] | (c[..., 1::2] << 4)).reshape(k // 512, 128, 2 * n)
    return np.ascontiguousarray(words), np.ascontiguousarray(byte.astype(np.uint8).reshape(k // 512, 16, n))


def unpack_weight(words, scales, fmt):
    g, _, n = scales.shape
    words = np.ascontiguousarray(words).reshape(g, 128, n, -1)
    if fmt == "e4m3":
        vals = words.view(ml_dtypes.float8_e4m3fn).astype(np.float64)
    else:
        nib = np.empty((g, 128, n, 4), np.uint8)
        nib[..., 0::2] = words & 0xF
        nib[..., 1::2] = words >> 4
        vals = E2M1[nib]
    vals = vals * np.repeat(np.exp2(scales.astype(np.float64) - 127.0), 8, axis=1)[..., None]
    return vals.transpose(0, 1, 3, 2).reshape(g * 512, n)


def gelu(v):
    return 0.5 * v * (1.0 + np.tanh(np.sqrt(2.0 / np.pi) * (v + 0.044715 * v**3)))


K, T, S, S2 = 1024, 2048, 512, 1024


def setup_inputs():
    n = np.random.standard_normal
    s = mx_kscale(K)[:, None]
    d = {}
    d["tab_words"], d["tab_scales"] = pack_weight(n((K, T)) * s, "e4m3")
    d["offs"] = striped(np.random.permutation(T)[:S])
    d["offs2"] = striped(np.random.permutation(T)[:S2])
    d["w1"] = (n((K, K)) / s / s.T / K).astype(np.float32)
    d["w4_words"], d["w4_scales"] = pack_weight(n((K, K)) / s / s.T / K, "e2m1")
    d["lean"] = (0.6 * n(S2)).astype(np.float32)
    return d


def reference(tab_words, tab_scales, offs, offs2, w1, w4_words, w4_scales, lean):
    TW = unpack_weight(tab_words, tab_scales, "e4m3")
    v = TW[:, unstriped(offs)]
    v2 = TW[:, unstriped(offs2)]
    w1q = mxq(f64(w1), 0, "e4m3")
    w4 = unpack_weight(w4_words, w4_scales, "e2m1")
    h = np.abs(w1q.T @ v)
    hq = mxq(h, 0, "e4m3")
    e = v2.T @ hq
    h2 = np.abs(w4.T @ v2)
    h2q = mxq(h2, 0, "e4m3")
    e2 = h2q.T @ v
    return np.tanh(e - e2 + f64(lean)[:, None])

@@ -1,0 +1,325 @@
+from contextlib import ExitStack
+
+import concourse.mybir as mybir
+
+K, T, S, S2 = 1024, 2048, 512, 1024
+P = 128
+PACK = 4
+KP = P * PACK
+PASSES = K // KP
+QUADS = 4
+GATHER = 256
+CAST_SPLIT = 80
+
+F32 = mybir.dt.float32
+BF16 = mybir.dt.bfloat16
+I32 = mybir.dt.int32
+U32 = mybir.dt.uint32
+U16 = mybir.dt.uint16
+U8 = mybir.dt.uint8
+E4M3 = mybir.dt.float8_e4m3fn_x4
+E2M1 = mybir.dt.float4_e2m1fn_x4
+ACT = mybir.ActivationFunctionType
+ALU = mybir.AluOpType
+
+FLOPS = 2 * K * K * S + 2 * K * K * S2 + 2 * 2 * K * S2 * S
+
+
+def tile_list_pairing_margins_kernel(tc, tab_words, tab_scales, offs, offs2, w1, w4_words, w4_scales, lean, out):
+    nc = tc.nc
+    with ExitStack() as ctx:
+        keep = ctx.enter_context(tc.tile_pool(name="keep", bufs=1))
+        psum = ctx.enter_context(tc.psum_pool(name="psum", bufs=8))
+
+        def held(shape, dtype, name):
+            return keep.tile(shape, dtype, name=name, align_bytes=64)
+
+        list1 = keep.tile([P, S // 16], U16, name="list1")
+        list2 = keep.tile([P, S2 // 16], U16, name="list2")
+        def staged(shape, dtype, name, slot):
+            return keep.tile(shape, dtype, name=name, tag="stage%d" % slot, align_bytes=64)
+
+        tab_w = {}
+        tab_s = held([P, T], U8, "tab_s")
+        w4_raw_w = [staged([P, 2 * K], U8, "w4_raw_w%d" % a, a) for a in range(PASSES)]
+        w4_raw_s = staged([P, PASSES * K], U8, "w4_raw_s", 2)
+        v2_s = held([P, S2], U8, "v2_s")
+        v2_s1 = held([P, S2], U8, "v2_s1")
+
+        nc.vector.memset(w4_raw_s[:].bitcast(I32), 0)
+        nc.gpsimd.memset(tab_s[:].bitcast(I32), 0)
+        nc.gpsimd.memset(v2_s1[:].bitcast(I32), 0)
+
+        def load_table_words(a, slot):
+            tab_w[a] = staged([P, T], U32, "tab_w%d" % a, slot)
+            nc.sync.dma_start(out=tab_w[a][:].bitcast(I32), in_=tab_words[a].rearrange("p n t -> p (n t)").bitcast(I32))
+
+        nc.sync.dma_start(list2[:], offs2)
+        for a in range(PASSES):
+            nc.sync.dma_start(out=w4_raw_w[a][:].bitcast(I32), in_=w4_words[a].bitcast(I32))
+        for q in range(QUADS):
+            nc.scalar.dma_start(
+                out=w4_raw_s[32 * q : 32 * q + 4, :].bitcast(I32),
+                in_=w4_scales[:, 4 * q : 4 * q + 4, :].rearrange("a r c -> r a c").bitcast(I32),
+            )
+        for q in range(QUADS):
+            nc.sync.dma_start(
+                out=tab_s[32 * q : 32 * q + 8, :].bitcast(I32),
+                in_=tab_scales[:, 4 * q : 4 * q + 4, :].bitcast(I32),
+            )
+        nc.sync.dma_start(list1[:], offs)
+        w1_raw = {}
+
+        def load_w1(a, b, slot):
+            w1_raw[a, b] = staged([P, PACK, KP], F32, "w1_raw%d%d" % (a, b), slot)
+            nc.sync.dma_start(
+                out=w1_raw[a, b][:],
+                in_=w1[KP * a : KP * (a + 1), KP * b : KP * (b + 1)].rearrange("(p j) c -> p j c", j=PACK),
+            )
+
+        w4_w = [held([P, 2 * K], U8, "w4_w%d" % a) for a in range(PASSES)]
+        w4_s = [held([P, K], U8, "w4_s%d" % a) for a in range(PASSES)]
+
+        def deal_w4_words(a):
+            nc.vector.tensor_copy(
+                out=w4_w[a][:].bitcast(U16).rearrange("p (b t m) -> p b t m", b=PASSES, t=PACK),
+                in_=w4_raw_w[a][:].bitcast(U16).rearrange("p (b m t) -> p b t m", b=PASSES, t=PACK),
+            )
+
+        def deal_w4_scales(a):
+            nc.vector.tensor_copy(
+                out=w4_s[a][:].rearrange("p (b t m) -> p b t m", b=PASSES, t=PACK),
+                in_=w4_raw_s[:, K * a : K * (a + 1)].rearrange("p (b m t) -> p b t m", b=PASSES, t=PACK),
+            )
+
+        def gather_v2_scales(g):
+            cols = GATHER // 16
+            nc.vector.tensor_copy(out=v2_s[:, g * GATHER : (g + 1) * GATHER], in_=tab_s[:].indirect(list2[:, cols * g : cols * (g + 1)]))
+
+        def lower_v2_scales():
+            for q in range(QUADS):
+                nc.scalar.dma_start(
+                    out=v2_s1[32 * q : 32 * q + 4, :].bitcast(I32),
+                    in_=v2_s[32 * q + 4 : 32 * q + 8, :].bitcast(I32),
+                )
+
+        v2_w = {}
+
+        def gather_v2_words(a, g):
+            v2_w[a, g] = held([P, GATHER], U32, "v2_w%d%d" % (a, g))
+            cols = GATHER // 16
+            nc.vector.tensor_copy(out=v2_w[a, g][:], in_=tab_w[a][:].indirect(list2[:, cols * g : cols * (g + 1)]))
+
+        def v2_operand(a, n):
+            g, i = divmod(n * P, GATHER)
+            plane = v2_s if a == 0 else v2_s1
+            return v2_w[a, g][:, i : i + P].bitcast(E4M3), plane[:, n * P : (n + 1) * P]
+
+        banks = {}
+
+        def fold2_pass(a, n):
+            words, plane = v2_operand(a, n)
+            for b in range(PASSES):
+                if a == 0:
+                    banks[n, b] = psum.tile([P, PACK * P], F32, name="bank")
+                for t in range(PACK):
+                    c = (b * PACK + t) * P
+                    nc.tensor.matmul_mx(
+                        out=banks[n, b][:, t * P : (t + 1) * P],
+                        lhsT=w4_w[a][:, 2 * c : 2 * (c + P)].bitcast(E2M1),
+                        lhsT_scale=w4_s[a][:, c : c + P],
+                        rhs=words,
+                        rhs_scale=plane,
+                        start=(a == 0 and t == 0),
+                        stop=(a == PASSES - 1 and t == PACK - 1),
+                    )
+
+        h2_bf = {}
+        h2_w = {}
+        h2_s = {}
+
+        def fold2_abs(n):
+            h2_bf[n] = staged([P, PASSES * KP], BF16, "h2_bf%d" % n, 4 + n)
+            for b in range(PASSES):
+                nc.scalar.activation(
+                    out=h2_bf[n][:, KP * b : KP * (b + 1)].rearrange("p (n t) -> p n t", t=PACK),
+                    in_=banks[n, b][:].rearrange("p (t n) -> p n t", t=PACK),
+                    func=ACT.Abs,
+                )
+
+        def fold2_quantize(n):
+            h2_w[n] = held([P, PASSES * P], U32, "h2_w%d" % n)
+            h2_s[n] = held([P, PASSES * P], U8, "h2_s%d" % n)
+            nc.vector.quantize_mx(out=h2_w[n][:].bitcast(E4M3), scales=h2_s[n][:], in_=h2_bf[n][:])
+
+        v1_w = {}
+        v1_planes = []
+
+        def gather_v1_scales(slot):
+            v1_planes.append(staged([P, S], U8, "v1_s", slot))
+            nc.vector.tensor_copy(out=v1_planes[0][:], in_=tab_s[:].indirect(list1[:]))
+
+        def gather_v1_words(a, slot):
+            v1_w[a] = staged([P, S], U32, "v1_w%d" % a, slot)
+            nc.vector.tensor_copy(out=v1_w[a][:], in_=tab_w[a][:].indirect(list1[:]))
+
+        w1_bf = {}
+        w1_w = {}
+        w1_s = {}
+
+        def cast_w1(a, b, split):
+            w1_bf[a, b] = staged([P, PACK * KP], BF16, "w1_bf%d%d" % (a, b), 12 + PASSES * b + a)
+            dst = w1_bf[a, b][:].rearrange("p (t m j) -> p m t j", t=PACK, j=PACK)
+            src = w1_raw[a, b][:].rearrange("p j (m t) -> p m t j", t=PACK)
+            if split > 0:
+                nc.vector.tensor_copy(out=dst[:, :split], in_=src[:, :split])
+            if split < P:
+                nc.scalar.copy(out=dst[:, split:], in_=src[:, split:])
+
+        def quantize_w1(a, b):
+            w1_w[a, b] = held([P, KP], U32, "w1_w%d%d" % (a, b))
+            w1_s[a, b] = held([P, KP], U8, "w1_s%d%d" % (a, b))
+            nc.vector.quantize_mx(out=w1_w[a, b][:].bitcast(E4M3), scales=w1_s[a, b][:], in_=w1_bf[a, b][:])
+
+        banks1 = {}
+
+        def fold1_pass(a, b, n):
+            if a == 0:
+                banks1[b, n] = psum.tile([P, PACK * P], F32, name="bank")
+            for t in range(PACK):
+                nc.tensor.matmul_mx(
+                    out=banks1[b, n][:, t * P : (t + 1) * P],
+                    lhsT=w1_w[a, b][:, t * P : (t + 1) * P].bitcast(E4M3),
+                    lhsT_scale=w1_s[a, b][:, t * P : (t + 1) * P],
+                    rhs=v1_w[a][:, n * P : (n + 1) * P].bitcast(E4M3),
+                    rhs_scale=v1_planes[0][4 * a : P, n * P : (n + 1) * P],
+                    start=(a == 0 and t == 0),
+                    stop=(a == PASSES - 1 and t == PACK - 1),
+                )
+
+        h_bf = [held([P, PACK * S], BF16, "h_bf%d" % b) for b in range(PASSES)]
+        hneg_bf = [held([P, PACK * S], BF16, "hneg_bf%d" % b) for b in range(PASSES)]
+        h_w = [held([P, S], U32, "h_w%d" % b) for b in range(PASSES)]
+        h_s = [held([P, S], U8, "h_s%d" % b) for b in range(PASSES)]
+
+        def fold1_abs(b, n):
+            nc.scalar.activation(
+                out=h_bf[b][:, KP * n : KP * (n + 1)].rearrange("p (n t) -> p n t", t=PACK),
+                in_=banks1[b, n][:].rearrange("p (t n) -> p n t", t=PACK),
+                func=ACT.Abs,
+            )
+
+        def fold1_negate(b, n):
+            cols = slice(KP * n, KP * (n + 1))
+            nc.vector.tensor_scalar(out=hneg_bf[b][:, cols], in0=h_bf[b][:, cols], scalar1=-1.0, scalar2=None, op0=ALU.mult)
+
+        def fold1_quantize(b, n):
+            nc.vector.quantize_mx(
+                out=h_w[b][:, n * P : (n + 1) * P].bitcast(E4M3),
+                scales=h_s[b][:, n * P : (n + 1) * P],
+                in_=hneg_bf[b][:, KP * n : KP * (n + 1)],
+            )
+
+        margins = {}
+
+        def match2(n):
+            margins[n] = psum.tile([P, S], F32, name="bank")
+            for b in range(PASSES):
+                nc.tensor.matmul_mx(
+                    out=margins[n][:],
+                    lhsT=h2_w[n][:, b * P : (b + 1) * P].bitcast(E4M3),
+                    lhsT_scale=h2_s[n][:, b * P : (b + 1) * P],
+                    rhs=v1_w[b][:].bitcast(E4M3),
+                    rhs_scale=v1_planes[0][4 * b : P, :],
+                    start=(b == 0),
+                    stop=False,
+                )
+
+        def match1(n, b):
+            words, plane = v2_operand(b, n)
+            nc.tensor.matmul_mx(
+                out=margins[n][:],
+                lhsT=words,
+                lhsT_scale=plane,
+                rhs=h_w[b][:].bitcast(E4M3),
+                rhs_scale=h_s[b][:],
+                start=False,
+                stop=(b == PASSES - 1),
+            )
+
+        def finish(n):
+            score = held([P, S], F32, "score%d" % n)
+            nc.scalar.activation(out=score[:], in_=margins[n][:], func=ACT.Tanh, scale=-1.0, bias=lean_t[:, n : n + 1])
+            nc.sync.dma_start(out=out[n * P : (n + 1) * P, :], in_=score[:])
+
+        tiles = S2 // P
+        half = tiles // 2
+        per = GATHER // P
+        groups = tiles // per
+        chunks = S // P
+        deal_w4_words(0)
+        load_table_words(0, 0)
+        deal_w4_words(1)
+        load_w1(0, 0, 1)
+        deal_w4_scales(0)
+        deal_w4_scales(1)
+        load_table_words(1, 2)
+        for g in range(groups):
+            gather_v2_scales(g)
+        lower_v2_scales()
+        for g in range(groups):
+            gather_v2_words(0, g)
+        for n in range(half):
+            fold2_pass(0, n)
+        cast_w1(0, 0, 0)
+        load_w1(1, 0, 1)
+        for g in range(groups):
+            gather_v2_words(1, g)
+        for n in range(half):
+            fold2_pass(1, n)
+            fold2_abs(n)
+        quantize_w1(0, 0)
+        gather_v1_words(1, 16)
+        gather_v1_scales(12)
+        fold2_quantize(0)
+        gather_v1_words(0, 4)
+        fold2_quantize(1)
+        load_w1(0, 1, 5)
+        fold2_quantize(2)
+        load_w1(1, 1, 6)
+        fold2_quantize(3)
+        for n in range(half, tiles):
+            for a in range(PASSES):
+                fold2_pass(a, n)
+            fold2_abs(n)
+            fold2_quantize(n)
+        cast_w1(1, 0, P)
+        quantize_w1(1, 0)
+        lean_t = staged([P, S2 // P], F32, "lean_t", 1)
+        with nc.allow_non_contiguous_dma(reason="one value a partition for each tile of 128 output rows"):
+            nc.sync.dma_start(out=lean_t[:], in_=lean.rearrange("(c p) -> p c", p=P))
+        for b in range(PASSES):
+            if b == 1:
+                cast_w1(0, 1, P)
+                quantize_w1(0, 1)
+                cast_w1(1, 1, CAST_SPLIT)
+                quantize_w1(1, 1)
+            for n in range(chunks):
+                for a in range(PASSES):
+                    fold1_pass(a, b, n)
+                fold1_abs(b, n)
+                fold1_negate(b, n)
+                fold1_quantize(b, n)
+            if b == 0:
+                for n in range(half):
+                    match2(n)
+                for n in range(half):
+                    match1(n, 0)
+        for n in range(half):
+            match1(n, 1)
+            finish(n)
+        for n in range(half, tiles):
+            match2(n)
+            for b in range(PASSES):
+                match1(n, b)
+            finish(n)

@@ -9,7 +9,6 @@ KP = P * PACK
 PASSES = K // KP
 QUADS = 4
 GATHER = 256
-CAST_SPLIT = 80
 
 F32 = mybir.dt.float32
 BF16 = mybir.dt.bfloat16
@@ -41,44 +40,51 @@ def tile_list_pairing_margins_kernel(tc, tab_words, tab_scales, offs, offs2, w1,
 
         tab_w = {}
         tab_s = held([P, T], U8, "tab_s")
-        w4_raw_w = [staged([P, 2 * K], U8, "w4_raw_w%d" % a, a) for a in range(PASSES)]
-        w4_raw_s = staged([P, PASSES * K], U8, "w4_raw_s", 2)
+        w4_raw_w = {}
+        w4_raw_s = staged([P, K], U8, "w4_raw_s", 1)
+        w4_s = [held([P, K], U8, "w4_s%d" % a) for a in range(PASSES)]
         v2_s = held([P, S2], U8, "v2_s")
         v2_s1 = held([P, S2], U8, "v2_s1")
 
-        nc.vector.memset(w4_raw_s[:].bitcast(I32), 0)
-        nc.gpsimd.memset(tab_s[:].bitcast(I32), 0)
+        nc.gpsimd.memset(w4_raw_s[:].bitcast(I32), 0)
+        nc.vector.memset(tab_s[:].bitcast(I32), 0)
+        nc.gpsimd.memset(w4_s[1][:].bitcast(I32), 0)
         nc.gpsimd.memset(v2_s1[:].bitcast(I32), 0)
 
         def load_table_words(a, slot):
             tab_w[a] = staged([P, T], U32, "tab_w%d" % a, slot)
             nc.sync.dma_start(out=tab_w[a][:].bitcast(I32), in_=tab_words[a].rearrange("p n t -> p (n t)").bitcast(I32))
 
-        nc.sync.dma_start(list2[:], offs2)
-        for a in range(PASSES):
+        def load_w4_words(a):
+            w4_raw_w[a] = staged([P, 2 * K], U8, "w4_raw_w%d" % a, 0)
             nc.sync.dma_start(out=w4_raw_w[a][:].bitcast(I32), in_=w4_words[a].bitcast(I32))
+
+        nc.sync.dma_start(list2[:], offs2)
+        load_w4_words(0)
+        load_table_words(0, 2)
+        nc.sync.dma_start(list1[:], offs)
         for q in range(QUADS):
             nc.scalar.dma_start(
-                out=w4_raw_s[32 * q : 32 * q + 4, :].bitcast(I32),
-                in_=w4_scales[:, 4 * q : 4 * q + 4, :].rearrange("a r c -> r a c").bitcast(I32),
+                out=w4_raw_s[32 * q : 32 * q + 8, :].bitcast(I32),
+                in_=w4_scales[:, 4 * q : 4 * q + 4, :].bitcast(I32),
             )
         for q in range(QUADS):
             nc.sync.dma_start(
                 out=tab_s[32 * q : 32 * q + 8, :].bitcast(I32),
                 in_=tab_scales[:, 4 * q : 4 * q + 4, :].bitcast(I32),
             )
-        nc.sync.dma_start(list1[:], offs)
         w1_raw = {}
 
-        def load_w1(a, b, slot):
-            w1_raw[a, b] = staged([P, PACK, KP], F32, "w1_raw%d%d" % (a, b), slot)
+        def load_w1(a, first, count, slot):
+            rows = staged([P, PACK, count * KP], F32, "w1_raw%d%d" % (a, first), slot)
             nc.sync.dma_start(
-                out=w1_raw[a, b][:],
-                in_=w1[KP * a : KP * (a + 1), KP * b : KP * (b + 1)].rearrange("(p j) c -> p j c", j=PACK),
+                out=rows[:],
+                in_=w1[KP * a : KP * (a + 1), KP * first : KP * (first + count)].rearrange("(p j) c -> p j c", j=PACK),
             )
+            for b in range(count):
+                w1_raw[a, first + b] = rows[:, :, KP * b : KP * (b + 1)]
 
         w4_w = [held([P, 2 * K], U8, "w4_w%d" % a) for a in range(PASSES)]
-        w4_s = [held([P, K], U8, "w4_s%d" % a) for a in range(PASSES)]
 
         def deal_w4_words(a):
             nc.vector.tensor_copy(
@@ -86,27 +92,26 @@ def tile_list_pairing_margins_kernel(tc, tab_words, tab_scales, offs, offs2, w1,
                 in_=w4_raw_w[a][:].bitcast(U16).rearrange("p (b m t) -> p b t m", b=PASSES, t=PACK),
             )
 
-        def deal_w4_scales(a):
+        def deal_w4_scales():
             nc.vector.tensor_copy(
-                out=w4_s[a][:].rearrange("p (b t m) -> p b t m", b=PASSES, t=PACK),
-                in_=w4_raw_s[:, K * a : K * (a + 1)].rearrange("p (b m t) -> p b t m", b=PASSES, t=PACK),
+                out=w4_s[0][:].rearrange("p (b t m) -> p b t m", b=PASSES, t=PACK),
+                in_=w4_raw_s[:].rearrange("p (b m t) -> p b t m", b=PASSES, t=PACK),
             )
 
-        def gather_v2_scales(g):
-            cols = GATHER // 16
-            nc.vector.tensor_copy(out=v2_s[:, g * GATHER : (g + 1) * GATHER], in_=tab_s[:].indirect(list2[:, cols * g : cols * (g + 1)]))
-
-        def lower_v2_scales():
+        def lower_plane(queue, low, packed):
             for q in range(QUADS):
-                nc.scalar.dma_start(
-                    out=v2_s1[32 * q : 32 * q + 4, :].bitcast(I32),
-                    in_=v2_s[32 * q + 4 : 32 * q + 8, :].bitcast(I32),
+                queue.dma_start(
+                    out=low[32 * q : 32 * q + 4, :].bitcast(I32),
+                    in_=packed[32 * q + 4 : 32 * q + 8, :].bitcast(I32),
                 )
+
+        def gather_v2_scales(first, last):
+            nc.vector.tensor_copy(out=v2_s[:, first:last], in_=tab_s[:].indirect(list2[:, first // 16 : last // 16]))
 
         v2_w = {}
 
-        def gather_v2_words(a, g):
-            v2_w[a, g] = held([P, GATHER], U32, "v2_w%d%d" % (a, g))
+        def gather_v2_words(a, g, slot):
+            v2_w[a, g] = staged([P, GATHER], U32, "v2_w%d%d" % (a, g), slot)
             cols = GATHER // 16
             nc.vector.tensor_copy(out=v2_w[a, g][:], in_=tab_w[a][:].indirect(list2[:, cols * g : cols * (g + 1)]))
 
@@ -139,10 +144,10 @@ def tile_list_pairing_margins_kernel(tc, tab_words, tab_scales, offs, offs2, w1,
         h2_s = {}
 
         def fold2_abs(n):
-            h2_bf[n] = staged([P, PASSES * KP], BF16, "h2_bf%d" % n, 4 + n)
             for b in range(PASSES):
+                h2_bf[n, b] = staged([P, KP], BF16, "h2_bf%d%d" % (n, b), 30 + PASSES * n + b)
                 nc.scalar.activation(
-                    out=h2_bf[n][:, KP * b : KP * (b + 1)].rearrange("p (n t) -> p n t", t=PACK),
+                    out=h2_bf[n, b][:].rearrange("p (n t) -> p n t", t=PACK),
                     in_=banks[n, b][:].rearrange("p (t n) -> p n t", t=PACK),
                     func=ACT.Abs,
                 )
@@ -150,7 +155,9 @@ def tile_list_pairing_margins_kernel(tc, tab_words, tab_scales, offs, offs2, w1,
         def fold2_quantize(n):
             h2_w[n] = held([P, PASSES * P], U32, "h2_w%d" % n)
             h2_s[n] = held([P, PASSES * P], U8, "h2_s%d" % n)
-            nc.vector.quantize_mx(out=h2_w[n][:].bitcast(E4M3), scales=h2_s[n][:], in_=h2_bf[n][:])
+            for b in range(PASSES):
+                cols = slice(b * P, (b + 1) * P)
+                nc.vector.quantize_mx(out=h2_w[n][:, cols].bitcast(E4M3), scales=h2_s[n][:, cols], in_=h2_bf[n, b][:])
 
         v1_w = {}
         v1_planes = []
@@ -170,7 +177,7 @@ def tile_list_pairing_margins_kernel(tc, tab_words, tab_scales, offs, offs2, w1,
         def cast_w1(a, b, split):
             w1_bf[a, b] = staged([P, PACK * KP], BF16, "w1_bf%d%d" % (a, b), 12 + PASSES * b + a)
             dst = w1_bf[a, b][:].rearrange("p (t m j) -> p m t j", t=PACK, j=PACK)
-            src = w1_raw[a, b][:].rearrange("p j (m t) -> p m t j", t=PACK)
+            src = w1_raw[a, b].rearrange("p j (m t) -> p m t j", t=PACK)
             if split > 0:
                 nc.vector.tensor_copy(out=dst[:, :split], in_=src[:, :split])
             if split < P:
@@ -257,64 +264,78 @@ def tile_list_pairing_margins_kernel(tc, tab_words, tab_scales, offs, offs2, w1,
         per = GATHER // P
         groups = tiles // per
         chunks = S // P
+
+        def fold1(b):
+            for a in range(PASSES):
+                for n in range(chunks):
+                    fold1_pass(a, b, n)
+            for n in range(chunks):
+                fold1_abs(b, n)
+
+        def fold1_codes(b):
+            for n in range(chunks):
+                fold1_negate(b, n)
+            for n in range(chunks):
+                fold1_quantize(b, n)
+
+        def fold2(g):
+            for n in range(g * per, (g + 1) * per):
+                for a in range(PASSES):
+                    fold2_pass(a, n)
+                fold2_abs(n)
+
         deal_w4_words(0)
-        load_table_words(0, 0)
-        deal_w4_words(1)
-        load_w1(0, 0, 1)
-        deal_w4_scales(0)
-        deal_w4_scales(1)
-        load_table_words(1, 2)
-        for g in range(groups):
-            gather_v2_scales(g)
-        lower_v2_scales()
-        for g in range(groups):
-            gather_v2_words(0, g)
+        load_w4_words(1)
+        deal_w4_scales()
+        load_table_words(1, 1)
+        lower_plane(nc.sync, w4_s[1], w4_s[0])
+        gather_v2_scales(0, GATHER)
+        for g in range(groups - 1):
+            gather_v2_words(0, g, 20 + g)
+        gather_v2_scales(GATHER, S2)
+        lower_plane(nc.scalar, v2_s1, v2_s)
         for n in range(half):
             fold2_pass(0, n)
-        cast_w1(0, 0, 0)
-        load_w1(1, 0, 1)
-        for g in range(groups):
-            gather_v2_words(1, g)
+        deal_w4_words(1)
+        load_w1(0, 0, 2, 0)
+        for g in range(groups - 1):
+            gather_v2_words(1, g, 23 + g)
         for n in range(half):
             fold2_pass(1, n)
             fold2_abs(n)
-        quantize_w1(0, 0)
-        gather_v1_words(1, 16)
-        gather_v1_scales(12)
+        fold2(2)
+        gather_v1_words(1, 26)
         fold2_quantize(0)
-        gather_v1_words(0, 4)
+        gather_v1_scales(30)
+        load_w1(1, 0, 1, 31)
         fold2_quantize(1)
-        load_w1(0, 1, 5)
-        fold2_quantize(2)
-        load_w1(1, 1, 6)
-        fold2_quantize(3)
-        for n in range(half, tiles):
-            for a in range(PASSES):
-                fold2_pass(a, n)
-            fold2_abs(n)
+        gather_v1_words(0, 32)
+        load_w1(1, 1, 1, 33)
+        for n in range(2, half):
             fold2_quantize(n)
-        cast_w1(1, 0, P)
-        quantize_w1(1, 0)
-        lean_t = staged([P, S2 // P], F32, "lean_t", 1)
+        for n in range(half):
+            match2(n)
+        for a in range(PASSES):
+            cast_w1(a, 0, P)
+            quantize_w1(a, 0)
+        cast_w1(0, 1, 0)
+        fold1(0)
+        gather_v2_words(0, 3, 31)
+        gather_v2_words(1, 3, 13)
+        fold2(3)
+        cast_w1(1, 1, P)
+        for a in range(PASSES):
+            quantize_w1(a, 1)
+        lean_t = staged([P, S2 // P], F32, "lean_t", 0)
         with nc.allow_non_contiguous_dma(reason="one value a partition for each tile of 128 output rows"):
             nc.sync.dma_start(out=lean_t[:], in_=lean.rearrange("(c p) -> p c", p=P))
-        for b in range(PASSES):
-            if b == 1:
-                cast_w1(0, 1, P)
-                quantize_w1(0, 1)
-                cast_w1(1, 1, CAST_SPLIT)
-                quantize_w1(1, 1)
-            for n in range(chunks):
-                for a in range(PASSES):
-                    fold1_pass(a, b, n)
-                fold1_abs(b, n)
-                fold1_negate(b, n)
-                fold1_quantize(b, n)
-            if b == 0:
-                for n in range(half):
-                    match2(n)
-                for n in range(half):
-                    match1(n, 0)
+        fold1(1)
+        fold1_codes(0)
+        for n in range(half):
+            match1(n, 0)
+        for n in range(half, tiles):
+            fold2_quantize(n)
+        fold1_codes(1)
         for n in range(half):
             match1(n, 1)
             finish(n)

@@ -98,11 +98,11 @@ def tile_list_pairing_margins_kernel(tc, tab_words, tab_scales, offs, offs2, w1,
                 in_=w4_raw_s[:].rearrange("p (b m t) -> p b t m", b=PASSES, t=PACK),
             )
 
-        def lower_plane(queue, low, packed):
+        def lower_plane(queue, low, packed, cols):
             for q in range(QUADS):
                 queue.dma_start(
-                    out=low[32 * q : 32 * q + 4, :].bitcast(I32),
-                    in_=packed[32 * q + 4 : 32 * q + 8, :].bitcast(I32),
+                    out=low[32 * q : 32 * q + 4, cols].bitcast(I32),
+                    in_=packed[32 * q + 4 : 32 * q + 8, cols].bitcast(I32),
                 )
 
         def gather_v2_scales(first, last):
@@ -144,10 +144,14 @@ def tile_list_pairing_margins_kernel(tc, tab_words, tab_scales, offs, offs2, w1,
         h2_s = {}
 
         def fold2_abs(n):
+            width = KP if n < 2 else PASSES * KP
+            h2_bf[n] = [
+                staged([P, width], BF16, "h2_bf%d%d" % (n, i), 30 + PASSES * n + i) for i in range(PASSES * KP // width)
+            ]
             for b in range(PASSES):
-                h2_bf[n, b] = staged([P, KP], BF16, "h2_bf%d%d" % (n, b), 30 + PASSES * n + b)
+                i, c = divmod(KP * b, width)
                 nc.scalar.activation(
-                    out=h2_bf[n, b][:].rearrange("p (n t) -> p n t", t=PACK),
+                    out=h2_bf[n][i][:, c : c + KP].rearrange("p (n t) -> p n t", t=PACK),
                     in_=banks[n, b][:].rearrange("p (t n) -> p n t", t=PACK),
                     func=ACT.Abs,
                 )
@@ -155,9 +159,10 @@ def tile_list_pairing_margins_kernel(tc, tab_words, tab_scales, offs, offs2, w1,
         def fold2_quantize(n):
             h2_w[n] = held([P, PASSES * P], U32, "h2_w%d" % n)
             h2_s[n] = held([P, PASSES * P], U8, "h2_s%d" % n)
-            for b in range(PASSES):
-                cols = slice(b * P, (b + 1) * P)
-                nc.vector.quantize_mx(out=h2_w[n][:, cols].bitcast(E4M3), scales=h2_s[n][:, cols], in_=h2_bf[n, b][:])
+            words = PASSES * P // len(h2_bf[n])
+            for i, values in enumerate(h2_bf[n]):
+                cols = slice(i * words, (i + 1) * words)
+                nc.vector.quantize_mx(out=h2_w[n][:, cols].bitcast(E4M3), scales=h2_s[n][:, cols], in_=values[:])
 
         v1_w = {}
         v1_planes = []
@@ -176,8 +181,8 @@ def tile_list_pairing_margins_kernel(tc, tab_words, tab_scales, offs, offs2, w1,
 
         def cast_w1(a, b, split):
             w1_bf[a, b] = staged([P, PACK * KP], BF16, "w1_bf%d%d" % (a, b), 12 + PASSES * b + a)
-            dst = w1_bf[a, b][:].rearrange("p (t m j) -> p m t j", t=PACK, j=PACK)
-            src = w1_raw[a, b].rearrange("p j (m t) -> p m t j", t=PACK)
+            dst = w1_bf[a, b][:].rearrange("p (t m j) -> p m j t", t=PACK, j=PACK)
+            src = w1_raw[a, b].rearrange("p j (m t) -> p m j t", t=PACK)
             if split > 0:
                 nc.vector.tensor_copy(out=dst[:, :split], in_=src[:, :split])
             if split < P:
@@ -217,14 +222,14 @@ def tile_list_pairing_margins_kernel(tc, tab_words, tab_scales, offs, offs2, w1,
             )
 
         def fold1_negate(b, n):
-            cols = slice(KP * n, KP * (n + 1))
+            cols = slice(2 * KP * n, 2 * KP * (n + 1))
             nc.vector.tensor_scalar(out=hneg_bf[b][:, cols], in0=h_bf[b][:, cols], scalar1=-1.0, scalar2=None, op0=ALU.mult)
 
         def fold1_quantize(b, n):
             nc.vector.quantize_mx(
-                out=h_w[b][:, n * P : (n + 1) * P].bitcast(E4M3),
-                scales=h_s[b][:, n * P : (n + 1) * P],
-                in_=hneg_bf[b][:, KP * n : KP * (n + 1)],
+                out=h_w[b][:, 2 * n * P : 2 * (n + 1) * P].bitcast(E4M3),
+                scales=h_s[b][:, 2 * n * P : 2 * (n + 1) * P],
+                in_=hneg_bf[b][:, 2 * KP * n : 2 * KP * (n + 1)],
             )
 
         margins = {}
@@ -256,8 +261,13 @@ def tile_list_pairing_margins_kernel(tc, tab_words, tab_scales, offs, offs2, w1,
 
         def finish(n):
             score = held([P, S], F32, "score%d" % n)
-            nc.scalar.activation(out=score[:], in_=margins[n][:], func=ACT.Tanh, scale=-1.0, bias=lean_t[:, n : n + 1])
-            nc.sync.dma_start(out=out[n * P : (n + 1) * P, :], in_=score[:])
+            width = S // 2 if n == S2 // P - 1 else S
+            for c in range(0, S, width):
+                cols = slice(c, c + width)
+                nc.scalar.activation(
+                    out=score[:, cols], in_=margins[n][:, cols], func=ACT.Tanh, scale=-1.0, bias=lean_t[:, n : n + 1]
+                )
+                nc.sync.dma_start(out=out[n * P : (n + 1) * P, cols], in_=score[:, cols])
 
         tiles = S2 // P
         half = tiles // 2
@@ -273,9 +283,9 @@ def tile_list_pairing_margins_kernel(tc, tab_words, tab_scales, offs, offs2, w1,
                 fold1_abs(b, n)
 
         def fold1_codes(b):
-            for n in range(chunks):
+            for n in range(chunks // 2):
                 fold1_negate(b, n)
-            for n in range(chunks):
+            for n in range(chunks // 2):
                 fold1_quantize(b, n)
 
         def fold2(g):
@@ -287,17 +297,19 @@ def tile_list_pairing_margins_kernel(tc, tab_words, tab_scales, offs, offs2, w1,
         deal_w4_words(0)
         load_w4_words(1)
         deal_w4_scales()
+        lower_plane(nc.sync, w4_s[1], w4_s[0], slice(0, K))
         load_table_words(1, 1)
-        lower_plane(nc.sync, w4_s[1], w4_s[0])
         gather_v2_scales(0, GATHER)
         for g in range(groups - 1):
             gather_v2_words(0, g, 20 + g)
-        gather_v2_scales(GATHER, S2)
-        lower_plane(nc.scalar, v2_s1, v2_s)
+        gather_v2_scales(GATHER, 2 * GATHER)
+        lower_plane(nc.scalar, v2_s1, v2_s, slice(0, S2 // 2))
         for n in range(half):
             fold2_pass(0, n)
         deal_w4_words(1)
         load_w1(0, 0, 2, 0)
+        gather_v2_scales(2 * GATHER, S2)
+        lower_plane(nc.scalar, v2_s1, v2_s, slice(S2 // 2, S2))
         for g in range(groups - 1):
             gather_v2_words(1, g, 23 + g)
         for n in range(half):

@@ -233,41 +233,50 @@ def tile_list_pairing_margins_kernel(tc, tab_words, tab_scales, offs, offs2, w1,
             )
 
         margins = {}
+        scores = {}
 
-        def match2(n):
-            margins[n] = psum.tile([P, S], F32, name="bank")
+        def match2(n, cols, acc, start):
             for b in range(PASSES):
                 nc.tensor.matmul_mx(
-                    out=margins[n][:],
+                    out=acc,
                     lhsT=h2_w[n][:, b * P : (b + 1) * P].bitcast(E4M3),
                     lhsT_scale=h2_s[n][:, b * P : (b + 1) * P],
-                    rhs=v1_w[b][:].bitcast(E4M3),
-                    rhs_scale=v1_planes[0][4 * b : P, :],
-                    start=(b == 0),
+                    rhs=v1_w[b][:, cols].bitcast(E4M3),
+                    rhs_scale=v1_planes[0][4 * b : P, cols],
+                    start=(start and b == 0),
                     stop=False,
                 )
 
-        def match1(n, b):
+        def match1(n, b, cols, acc, stop):
             words, plane = v2_operand(b, n)
             nc.tensor.matmul_mx(
-                out=margins[n][:],
+                out=acc,
                 lhsT=words,
                 lhsT_scale=plane,
-                rhs=h_w[b][:].bitcast(E4M3),
-                rhs_scale=h_s[b][:],
+                rhs=h_w[b][:, cols].bitcast(E4M3),
+                rhs_scale=h_s[b][:, cols],
                 start=False,
-                stop=(b == PASSES - 1),
+                stop=stop,
             )
 
-        def finish(n):
-            score = held([P, S], F32, "score%d" % n)
-            width = S // 2 if n == S2 // P - 1 else S
-            for c in range(0, S, width):
-                cols = slice(c, c + width)
-                nc.scalar.activation(
-                    out=score[:, cols], in_=margins[n][:, cols], func=ACT.Tanh, scale=-1.0, bias=lean_t[:, n : n + 1]
-                )
-                nc.sync.dma_start(out=out[n * P : (n + 1) * P, cols], in_=score[:, cols])
+        def finish(n, cols, acc):
+            if n not in scores:
+                scores[n] = held([P, S], F32, "score%d" % n)
+            nc.scalar.activation(out=scores[n][:, cols], in_=acc, func=ACT.Tanh, scale=-1.0, bias=lean_t[:, n : n + 1])
+            nc.sync.dma_start(out=out[n * P : (n + 1) * P, cols], in_=scores[n][:, cols])
+
+        sides = [slice(0, S // 2), slice(S // 2, S)]
+        whole = slice(0, S)
+
+        def early_margin(n, u):
+            if (n // 2, u) not in margins:
+                margins[n // 2, u] = psum.tile([P, S], F32, name="bank")
+            return margins[n // 2, u][:, sides[n % 2]]
+
+        def late_margin(n):
+            margins[n] = psum.tile([P, S], F32, name="bank")
+            match2(n, whole, margins[n][:], True)
+            match1(n, 0, whole, margins[n][:], False)
 
         tiles = S2 // P
         half = tiles // 2
@@ -326,7 +335,8 @@ def tile_list_pairing_margins_kernel(tc, tab_words, tab_scales, offs, offs2, w1,
         for n in range(2, half):
             fold2_quantize(n)
         for n in range(half):
-            match2(n)
+            for u in range(2):
+                match2(n, sides[u], early_margin(n, u), n % 2 == 0)
         for a in range(PASSES):
             cast_w1(a, 0, P)
             quantize_w1(a, 0)
@@ -344,15 +354,20 @@ def tile_list_pairing_margins_kernel(tc, tab_words, tab_scales, offs, offs2, w1,
         fold1(1)
         fold1_codes(0)
         for n in range(half):
-            match1(n, 0)
+            for u in range(2):
+                match1(n, 0, sides[u], early_margin(n, u), False)
         for n in range(half, tiles):
             fold2_quantize(n)
         fold1_codes(1)
-        for n in range(half):
-            match1(n, 1)
-            finish(n)
+        for u in range(2):
+            late_margin(half + u)
+            for n in range(half):
+                match1(n, 1, sides[u], early_margin(n, u), n % 2 == 1)
+            for n in range(half):
+                finish(n, sides[u], early_margin(n, u))
         for n in range(half, tiles):
-            match2(n)
-            for b in range(PASSES):
-                match1(n, b)
-            finish(n)
+            if n >= half + 2:
+                late_margin(n)
+            match1(n, 1, whole, margins[n][:], True)
+            for cols in sides if n == tiles - 1 else [whole]:
+                finish(n, cols, margins[n][:, cols])

from contextlib import ExitStack

import concourse.mybir as mybir

K, T, S, S2 = 1024, 2048, 512, 1024
P = 128
PACK = 4
KP = P * PACK
PASSES = K // KP
QUADS = 4
GATHER = 256

F32 = mybir.dt.float32
BF16 = mybir.dt.bfloat16
I32 = mybir.dt.int32
U32 = mybir.dt.uint32
U16 = mybir.dt.uint16
U8 = mybir.dt.uint8
E4M3 = mybir.dt.float8_e4m3fn_x4
E2M1 = mybir.dt.float4_e2m1fn_x4
ACT = mybir.ActivationFunctionType
ALU = mybir.AluOpType

FLOPS = 2 * K * K * S + 2 * K * K * S2 + 2 * 2 * K * S2 * S


def tile_list_pairing_margins_kernel(tc, tab_words, tab_scales, offs, offs2, w1, w4_words, w4_scales, lean, out):
    nc = tc.nc
    with ExitStack() as ctx:
        keep = ctx.enter_context(tc.tile_pool(name="keep", bufs=1))
        psum = ctx.enter_context(tc.psum_pool(name="psum", bufs=8))

        def held(shape, dtype, name):
            return keep.tile(shape, dtype, name=name, align_bytes=64)

        list1 = keep.tile([P, S // 16], U16, name="list1")
        list2 = keep.tile([P, S2 // 16], U16, name="list2")
        def staged(shape, dtype, name, slot):
            return keep.tile(shape, dtype, name=name, tag="stage%d" % slot, align_bytes=64)

        tab_w = {}
        tab_s = held([P, T], U8, "tab_s")
        w4_raw_w = {}
        w4_raw_s = staged([P, K], U8, "w4_raw_s", 1)
        w4_s = [held([P, K], U8, "w4_s%d" % a) for a in range(PASSES)]
        v2_s = held([P, S2], U8, "v2_s")
        v2_s1 = held([P, S2], U8, "v2_s1")

        nc.gpsimd.memset(w4_raw_s[:].bitcast(I32), 0)
        nc.vector.memset(tab_s[:].bitcast(I32), 0)
        nc.gpsimd.memset(w4_s[1][:].bitcast(I32), 0)
        nc.gpsimd.memset(v2_s1[:].bitcast(I32), 0)

        def load_table_words(a, slot):
            tab_w[a] = staged([P, T], U32, "tab_w%d" % a, slot)
            nc.sync.dma_start(out=tab_w[a][:].bitcast(I32), in_=tab_words[a].rearrange("p n t -> p (n t)").bitcast(I32))

        def load_w4_words(a):
            w4_raw_w[a] = staged([P, 2 * K], U8, "w4_raw_w%d" % a, 0)
            nc.sync.dma_start(out=w4_raw_w[a][:].bitcast(I32), in_=w4_words[a].bitcast(I32))

        nc.sync.dma_start(list2[:], offs2)
        load_w4_words(0)
        load_table_words(0, 2)
        nc.sync.dma_start(list1[:], offs)
        for q in range(QUADS):
            nc.scalar.dma_start(
                out=w4_raw_s[32 * q : 32 * q + 8, :].bitcast(I32),
                in_=w4_scales[:, 4 * q : 4 * q + 4, :].bitcast(I32),
            )
        for q in range(QUADS):
            nc.sync.dma_start(
                out=tab_s[32 * q : 32 * q + 8, :].bitcast(I32),
                in_=tab_scales[:, 4 * q : 4 * q + 4, :].bitcast(I32),
            )
        w1_raw = {}

        def load_w1(a, first, count, slot):
            rows = staged([P, PACK, count * KP], F32, "w1_raw%d%d" % (a, first), slot)
            nc.sync.dma_start(
                out=rows[:],
                in_=w1[KP * a : KP * (a + 1), KP * first : KP * (first + count)].rearrange("(p j) c -> p j c", j=PACK),
            )
            for b in range(count):
                w1_raw[a, first + b] = rows[:, :, KP * b : KP * (b + 1)]

        w4_w = [held([P, 2 * K], U8, "w4_w%d" % a) for a in range(PASSES)]

        def deal_w4_words(a):
            nc.vector.tensor_copy(
                out=w4_w[a][:].bitcast(U16).rearrange("p (b t m) -> p b t m", b=PASSES, t=PACK),
                in_=w4_raw_w[a][:].bitcast(U16).rearrange("p (b m t) -> p b t m", b=PASSES, t=PACK),
            )

        def deal_w4_scales():
            nc.vector.tensor_copy(
                out=w4_s[0][:].rearrange("p (b t m) -> p b t m", b=PASSES, t=PACK),
                in_=w4_raw_s[:].rearrange("p (b m t) -> p b t m", b=PASSES, t=PACK),
            )

        def lower_plane(queue, low, packed, cols):
            for q in range(QUADS):
                queue.dma_start(
                    out=low[32 * q : 32 * q + 4, cols].bitcast(I32),
                    in_=packed[32 * q + 4 : 32 * q + 8, cols].bitcast(I32),
                )

        def gather_v2_scales(first, last):
            nc.vector.tensor_copy(out=v2_s[:, first:last], in_=tab_s[:].indirect(list2[:, first // 16 : last // 16]))

        v2_w = {}

        def gather_v2_words(a, g, slot):
            v2_w[a, g] = staged([P, GATHER], U32, "v2_w%d%d" % (a, g), slot)
            cols = GATHER // 16
            nc.vector.tensor_copy(out=v2_w[a, g][:], in_=tab_w[a][:].indirect(list2[:, cols * g : cols * (g + 1)]))

        def v2_operand(a, n):
            g, i = divmod(n * P, GATHER)
            plane = v2_s if a == 0 else v2_s1
            return v2_w[a, g][:, i : i + P].bitcast(E4M3), plane[:, n * P : (n + 1) * P]

        banks = {}

        def fold2_pass(a, n):
            words, plane = v2_operand(a, n)
            for b in range(PASSES):
                if a == 0:
                    banks[n, b] = psum.tile([P, PACK * P], F32, name="bank")
                for t in range(PACK):
                    c = (b * PACK + t) * P
                    nc.tensor.matmul_mx(
                        out=banks[n, b][:, t * P : (t + 1) * P],
                        lhsT=w4_w[a][:, 2 * c : 2 * (c + P)].bitcast(E2M1),
                        lhsT_scale=w4_s[a][:, c : c + P],
                        rhs=words,
                        rhs_scale=plane,
                        start=(a == 0 and t == 0),
                        stop=(a == PASSES - 1 and t == PACK - 1),
                    )

        h2_bf = {}
        h2_w = {}
        h2_s = {}

        def fold2_abs(n):
            width = KP if n < 2 else PASSES * KP
            h2_bf[n] = [
                staged([P, width], BF16, "h2_bf%d%d" % (n, i), 30 + PASSES * n + i) for i in range(PASSES * KP // width)
            ]
            for b in range(PASSES):
                i, c = divmod(KP * b, width)
                nc.scalar.activation(
                    out=h2_bf[n][i][:, c : c + KP].rearrange("p (n t) -> p n t", t=PACK),
                    in_=banks[n, b][:].rearrange("p (t n) -> p n t", t=PACK),
                    func=ACT.Abs,
                )

        def fold2_quantize(n):
            h2_w[n] = held([P, PASSES * P], U32, "h2_w%d" % n)
            h2_s[n] = held([P, PASSES * P], U8, "h2_s%d" % n)
            words = PASSES * P // len(h2_bf[n])
            for i, values in enumerate(h2_bf[n]):
                cols = slice(i * words, (i + 1) * words)
                nc.vector.quantize_mx(out=h2_w[n][:, cols].bitcast(E4M3), scales=h2_s[n][:, cols], in_=values[:])

        v1_w = {}
        v1_planes = []

        def gather_v1_scales(slot):
            v1_planes.append(staged([P, S], U8, "v1_s", slot))
            nc.vector.tensor_copy(out=v1_planes[0][:], in_=tab_s[:].indirect(list1[:]))

        def gather_v1_words(a, slot):
            v1_w[a] = staged([P, S], U32, "v1_w%d" % a, slot)
            nc.vector.tensor_copy(out=v1_w[a][:], in_=tab_w[a][:].indirect(list1[:]))

        w1_bf = {}
        w1_w = {}
        w1_s = {}

        def cast_w1(a, b, split):
            w1_bf[a, b] = staged([P, PACK * KP], BF16, "w1_bf%d%d" % (a, b), 12 + PASSES * b + a)
            dst = w1_bf[a, b][:].rearrange("p (t m j) -> p m j t", t=PACK, j=PACK)
            src = w1_raw[a, b].rearrange("p j (m t) -> p m j t", t=PACK)
            if split > 0:
                nc.vector.tensor_copy(out=dst[:, :split], in_=src[:, :split])
            if split < P:
                nc.scalar.copy(out=dst[:, split:], in_=src[:, split:])

        def quantize_w1(a, b):
            w1_w[a, b] = held([P, KP], U32, "w1_w%d%d" % (a, b))
            w1_s[a, b] = held([P, KP], U8, "w1_s%d%d" % (a, b))
            nc.vector.quantize_mx(out=w1_w[a, b][:].bitcast(E4M3), scales=w1_s[a, b][:], in_=w1_bf[a, b][:])

        banks1 = {}

        def fold1_pass(a, b, n):
            if a == 0:
                banks1[b, n] = psum.tile([P, PACK * P], F32, name="bank")
            for t in range(PACK):
                nc.tensor.matmul_mx(
                    out=banks1[b, n][:, t * P : (t + 1) * P],
                    lhsT=w1_w[a, b][:, t * P : (t + 1) * P].bitcast(E4M3),
                    lhsT_scale=w1_s[a, b][:, t * P : (t + 1) * P],
                    rhs=v1_w[a][:, n * P : (n + 1) * P].bitcast(E4M3),
                    rhs_scale=v1_planes[0][4 * a : P, n * P : (n + 1) * P],
                    start=(a == 0 and t == 0),
                    stop=(a == PASSES - 1 and t == PACK - 1),
                )

        h_bf = [held([P, PACK * S], BF16, "h_bf%d" % b) for b in range(PASSES)]
        hneg_bf = [held([P, PACK * S], BF16, "hneg_bf%d" % b) for b in range(PASSES)]
        h_w = [held([P, S], U32, "h_w%d" % b) for b in range(PASSES)]
        h_s = [held([P, S], U8, "h_s%d" % b) for b in range(PASSES)]

        def fold1_abs(b, n):
            nc.scalar.activation(
                out=h_bf[b][:, KP * n : KP * (n + 1)].rearrange("p (n t) -> p n t", t=PACK),
                in_=banks1[b, n][:].rearrange("p (t n) -> p n t", t=PACK),
                func=ACT.Abs,
            )

        def fold1_negate(b, n):
            cols = slice(2 * KP * n, 2 * KP * (n + 1))
            nc.vector.tensor_scalar(out=hneg_bf[b][:, cols], in0=h_bf[b][:, cols], scalar1=-1.0, scalar2=None, op0=ALU.mult)

        def fold1_quantize(b, n):
            nc.vector.quantize_mx(
                out=h_w[b][:, 2 * n * P : 2 * (n + 1) * P].bitcast(E4M3),
                scales=h_s[b][:, 2 * n * P : 2 * (n + 1) * P],
                in_=hneg_bf[b][:, 2 * KP * n : 2 * KP * (n + 1)],
            )

        margins = {}
        scores = {}

        def match2(n, cols, acc, start):
            for b in range(PASSES):
                nc.tensor.matmul_mx(
                    out=acc,
                    lhsT=h2_w[n][:, b * P : (b + 1) * P].bitcast(E4M3),
                    lhsT_scale=h2_s[n][:, b * P : (b + 1) * P],
                    rhs=v1_w[b][:, cols].bitcast(E4M3),
                    rhs_scale=v1_planes[0][4 * b : P, cols],
                    start=(start and b == 0),
                    stop=False,
                )

        def match1(n, b, cols, acc, stop):
            words, plane = v2_operand(b, n)
            nc.tensor.matmul_mx(
                out=acc,
                lhsT=words,
                lhsT_scale=plane,
                rhs=h_w[b][:, cols].bitcast(E4M3),
                rhs_scale=h_s[b][:, cols],
                start=False,
                stop=stop,
            )

        def finish(n, cols, acc):
            if n not in scores:
                scores[n] = held([P, S], F32, "score%d" % n)
            nc.scalar.activation(out=scores[n][:, cols], in_=acc, func=ACT.Tanh, scale=-1.0, bias=lean_t[:, n : n + 1])
            nc.sync.dma_start(out=out[n * P : (n + 1) * P, cols], in_=scores[n][:, cols])

        sides = [slice(0, S // 2), slice(S // 2, S)]
        whole = slice(0, S)

        def early_margin(n, u):
            if (n // 2, u) not in margins:
                margins[n // 2, u] = psum.tile([P, S], F32, name="bank")
            return margins[n // 2, u][:, sides[n % 2]]

        def late_margin(n):
            margins[n] = psum.tile([P, S], F32, name="bank")
            match2(n, whole, margins[n][:], True)
            match1(n, 0, whole, margins[n][:], False)

        tiles = S2 // P
        half = tiles // 2
        per = GATHER // P
        groups = tiles // per
        chunks = S // P

        def fold1(b):
            for a in range(PASSES):
                for n in range(chunks):
                    fold1_pass(a, b, n)
            for n in range(chunks):
                fold1_abs(b, n)

        def fold1_codes(b):
            for n in range(chunks // 2):
                fold1_negate(b, n)
            for n in range(chunks // 2):
                fold1_quantize(b, n)

        def fold2(g):
            for n in range(g * per, (g + 1) * per):
                for a in range(PASSES):
                    fold2_pass(a, n)
                fold2_abs(n)

        deal_w4_words(0)
        load_w4_words(1)
        deal_w4_scales()
        lower_plane(nc.sync, w4_s[1], w4_s[0], slice(0, K))
        load_table_words(1, 1)
        gather_v2_scales(0, GATHER)
        for g in range(groups - 1):
            gather_v2_words(0, g, 20 + g)
        gather_v2_scales(GATHER, 2 * GATHER)
        lower_plane(nc.scalar, v2_s1, v2_s, slice(0, S2 // 2))
        for n in range(half):
            fold2_pass(0, n)
        deal_w4_words(1)
        load_w1(0, 0, 2, 0)
        gather_v2_scales(2 * GATHER, S2)
        lower_plane(nc.scalar, v2_s1, v2_s, slice(S2 // 2, S2))
        for g in range(groups - 1):
            gather_v2_words(1, g, 23 + g)
        for n in range(half):
            fold2_pass(1, n)
            fold2_abs(n)
        fold2(2)
        gather_v1_words(1, 26)
        fold2_quantize(0)
        gather_v1_scales(30)
        load_w1(1, 0, 1, 31)
        fold2_quantize(1)
        gather_v1_words(0, 32)
        load_w1(1, 1, 1, 33)
        for n in range(2, half):
            fold2_quantize(n)
        for n in range(half):
            for u in range(2):
                match2(n, sides[u], early_margin(n, u), n % 2 == 0)
        for a in range(PASSES):
            cast_w1(a, 0, P)
            quantize_w1(a, 0)
        cast_w1(0, 1, 0)
        fold1(0)
        gather_v2_words(0, 3, 31)
        gather_v2_words(1, 3, 13)
        fold2(3)
        cast_w1(1, 1, P)
        for a in range(PASSES):
            quantize_w1(a, 1)
        lean_t = staged([P, S2 // P], F32, "lean_t", 0)
        with nc.allow_non_contiguous_dma(reason="one value a partition for each tile of 128 output rows"):
            nc.sync.dma_start(out=lean_t[:], in_=lean.rearrange("(c p) -> p c", p=P))
        fold1(1)
        fold1_codes(0)
        for n in range(half):
            for u in range(2):
                match1(n, 0, sides[u], early_margin(n, u), False)
        for n in range(half, tiles):
            fold2_quantize(n)
        fold1_codes(1)
        for u in range(2):
            late_margin(half + u)
            for n in range(half):
                match1(n, 1, sides[u], early_margin(n, u), n % 2 == 1)
            for n in range(half):
                finish(n, sides[u], early_margin(n, u))
        for n in range(half, tiles):
            if n >= half + 2:
                late_margin(n)
            match1(n, 1, whole, margins[n][:], True)
            for cols in sides if n == tiles - 1 else [whole]:
                finish(n, cols, margins[n][:, cols])
